import numpy as np
import ml_dtypes


def mxq(x, axis, fmt="e4m3"):
    dtype, down = {"e4m3": (ml_dtypes.float8_e4m3fn, 7), "e5m2": (ml_dtypes.float8_e5m2, 14)}[fmt]
    v = np.moveaxis(np.asarray(x, np.float32).astype(ml_dtypes.bfloat16).astype(np.float64), axis, -1)
    blocks = v.reshape(v.shape[:-1] + (-1, 32))
    amax = np.abs(blocks).max(-1, keepdims=True)
    byte = np.maximum(np.where(amax > 0, np.frexp(amax)[1] - 1 + 127, 0) - down, 1)
    scale = np.exp2(byte - 127.0)
    codes = (blocks / scale).astype(np.float32).astype(dtype).astype(np.float64)
    return np.moveaxis((codes * scale).reshape(v.shape), -1, axis)


WIDE = False


def mx_kscale(k):
    if not WIDE:
        return np.ones(k)
    levels = np.array([10, -10, 5, -5, 0])
    if k % 512:
        return np.exp2(np.random.permutation(np.resize(levels, k // 32))).repeat(32)
    a = np.empty((k // 512, 16))
    for p in range(k // 512):
        a[p, :8] = np.random.permutation(np.resize(levels, 8))
        for g in range(8):
            far = levels[np.abs(levels - a[p, g]) >= 10]
            a[p, g + 8] = far[np.random.randint(len(far))]
    return np.exp2(a.ravel()).repeat(32)


def f64(x):
    return np.asarray(x).astype(np.float64)


def striped(idx):
    return np.tile(idx.reshape(-1, 16).T, (8, 1)).astype(np.uint16)


def unstriped(offs):
    return offs[:16].T.reshape(-1).astype(np.int64)


def striped8(idx):
    return np.concatenate([x.reshape(-1, 16).T for x in idx]).astype(np.uint16)


def runs(offs, k):
    lists = np.stack([offs[16 * r : 16 * r + 16].T.reshape(-1) for r in range(8)]).astype(np.int64)
    return lists[np.arange(k) % 512 // 64]


def pack_weight(w):
    k, n = w.shape
    w = f64(np.asarray(w, np.float32).astype(ml_dtypes.bfloat16)).reshape(k // 32, 32, n)
    amax = np.abs(w).max(1)
    byte = np.clip(np.where(amax > 0, np.frexp(amax)[1] - 1 + 127 - 7, 1), 1, 254)
    scaled = (w * np.exp2(127.0 - byte)[:, None, :]).reshape(k, n).astype(np.float32)
    words = np.ascontiguousarray(scaled.reshape(k // 512, 128, 4, n).transpose(0, 1, 3, 2)).astype(ml_dtypes.float8_e4m3fn).view(np.uint8)
    return words, np.ascontiguousarray(byte.astype(np.uint8).reshape(k // 512, 16, n))


def unpack_weight(words, scales):
    g, p, n, _ = words.shape
    vals = np.ascontiguousarray(words).view(ml_dtypes.float8_e4m3fn).astype(np.float64) * np.repeat(np.exp2(scales.astype(np.float64) - 127.0), 8, axis=1)[..., None]
    return vals.transpose(0, 1, 3, 2).reshape(g * 512, n)


K, T, S, V, N, H = 512, 2048, 1024, 512, 512, 512


def setup_inputs():
    n = np.random.standard_normal
    s = mx_kscale(K)[:, None]
    u = mx_kscale(H)
    packed_xT = pack_weight(n((K, T)) * s)
    return {
        "x_words": packed_xT[0],
        "x_scales": packed_xT[1],
        "w1": (n((K, H)) / np.sqrt(K) / s * u).astype(np.float32),
        "w2": (n((K, H)) / np.sqrt(K) / s * u).astype(np.float32),
        "cw": n((H, V)).astype(np.float32),
        "sw": n((H, V)).astype(np.float32),
        "w3": (n((H, N)) / np.sqrt(2 * H) / u[:, None]).astype(np.float32),
        "w4": (n((H, N)) / np.sqrt(2 * H) / u[:, None]).astype(np.float32),
        "offs": striped(np.random.permutation(T)[:S]),
        "left": striped8(np.stack([np.random.permutation(S)[:V] for _ in range(8)])),
        "right": striped8(np.stack([np.random.permutation(S)[:V] for _ in range(8)])),
    }


def reference(x_words, x_scales, w1, w2, cw, sw, w3, w4, offs, left, right):
    xq = unpack_weight(x_words, x_scales)[:, unstriped(offs)]
    y = mxq(f64(w1), 0, "e4m3").T @ xq
    yr = y[np.arange(H)[:, None], runs(right, H)]
    e = mxq(f64(w2), 0, "e4m3").T @ xq
    er = e[np.arange(H)[:, None], runs(right, H)]
    z = y[np.arange(H)[:, None], runs(left, H)] + f64(cw) * yr - (f64(sw) * er)
    z2 = e[np.arange(H)[:, None], runs(left, H)] + f64(sw) * yr + f64(cw) * er
    return mxq(f64(w3), 0, "e4m3").T @ mxq(z, 0, "e4m3") + mxq(f64(w4), 0, "e4m3").T @ mxq(z2, 0, "e4m3")

@@ -1,0 +1,279 @@
+from contextlib import ExitStack
+
+import concourse.mybir as mybir
+from concourse.masks import make_identity
+
+F32 = mybir.dt.float32
+BF16 = mybir.dt.bfloat16
+I32 = mybir.dt.int32
+U32 = mybir.dt.uint32
+U16 = mybir.dt.uint16
+U8 = mybir.dt.uint8
+FP8X4 = mybir.dt.float8_e4m3fn_x4
+MULT = mybir.AluOpType.mult
+ADD = mybir.AluOpType.add
+SUB = mybir.AluOpType.subtract
+
+P = 128
+PACK = 4
+K, T, S, V, N, H = 512, 2048, 1024, 512, 512, 512
+BANK = 512
+HALF = V // 2
+FLOPS = 2 * (2 * K * H * S) + 2 * (2 * H * N * V)
+
+
+def tile_picked_cbutter_none_p_kernel(
+    tc, x_words, x_scales, w1, w2, cw, sw, w3, w4, offs, left, right, out
+):
+    nc = tc.nc
+    with ExitStack() as ctx:
+        lists = ctx.enter_context(tc.tile_pool(name="lists", bufs=1))
+        keep = ctx.enter_context(tc.tile_pool(name="keep", bufs=1))
+        psum = ctx.enter_context(tc.psum_pool(name="psum", bufs=1))
+
+        def sb(name, shape, dtype):
+            return keep.tile(shape, dtype, name=name, align_bytes=64)
+
+        banks = [psum.tile([P, BANK], F32, name="bank%d" % b) for b in range(8)]
+
+        offs_sb = lists.tile([P, S // 16], U16, name="offs_sb")
+        right_sb = lists.tile([P, V // 16], U16, name="right_sb")
+        left_sb = lists.tile([P, V // 16], U16, name="left_sb")
+        scale_table = sb("scale_table", [P, T], U8)
+        word_table = sb("word_table", [P, T], I32)
+        nc.sync.dma_start(offs_sb[:], offs)
+        for quad in range(4):
+            nc.sync.dma_start(
+                out=scale_table[32 * quad : 32 * quad + 32, :].bitcast(I32),
+                in_=x_scales[0, 4 * quad : 4 * quad + 4, :].bitcast(I32).unsqueeze(0).to_broadcast([8, 4, T // 4]),
+            )
+
+        def load_weight(name, w):
+            raw = sb(name, [P, PACK, w.shape[1]], F32)
+            nc.sync.dma_start(out=raw[:], in_=w.rearrange("(p j) c -> p j c", j=PACK))
+            return raw
+
+        w1_raw = load_weight("w1_raw", w1)
+        nc.sync.dma_start(out=word_table[:], in_=x_words[0].rearrange("p n j -> p (n j)").bitcast(I32))
+        w2_raw = load_weight("w2_raw", w2)
+        nc.sync.dma_start(right_sb[:], right)
+        nc.sync.dma_start(left_sb[:], left)
+        cw_sb, sw_sb = [], []
+        for first, count in ((0, 1), (1, 1), (2, 2)):
+            for name, src, tiles in (("cw", cw, cw_sb), ("sw", sw, sw_sb)):
+                rows = sb("%s%d" % (name, first), [P, count, V], F32)
+                nc.sync.dma_start(out=rows[:], in_=src.rearrange("(p t) v -> p t v", t=PACK)[:, first : first + count, :])
+                tiles.extend(rows[:, i, :] for i in range(count))
+        w3_raw = load_weight("w3_raw", w3)
+        w4_raw = load_weight("w4_raw", w4)
+
+        identity = sb("identity", [P, P], F32)
+        make_identity(nc, identity[:])
+
+        def quantize(name, grouped):
+            width = grouped.shape[1] // PACK
+            codes = sb(name + "_codes", [P, width], U32)
+            scales = sb(name + "_scales", [P, width], U8)
+            nc.vector.quantize_mx(out=codes[:].bitcast(FP8X4), scales=scales[:], in_=grouped)
+            return codes, scales
+
+        def group_dealt(name, raw):
+            grouped = sb(name + "_bf16", [P, H * PACK], BF16)
+            nc.scalar.copy(
+                out=grouped[:].rearrange("p (t m j) -> p m j t", t=PACK, j=PACK),
+                in_=raw[:].rearrange("p j (m t) -> p m j t", t=PACK),
+            )
+            return grouped
+
+        def group_plain(name, raw):
+            grouped = sb(name + "_bf16", [P, N * PACK], BF16)
+            nc.scalar.copy(
+                out=grouped[:].rearrange("p (c i j) -> p c j i", i=4, j=PACK),
+                in_=raw[:].rearrange("p j (c i) -> p c j i", i=4),
+            )
+            return grouped
+
+        picked_scales = sb("picked_scales", [P, S], U8)
+        nc.vector.tensor_copy(picked_scales[:], scale_table[:].indirect(offs_sb[:]))
+        w1_q = quantize("w1", group_dealt("w1", w1_raw)[:])
+        picked_words = []
+        for c in range(S // BANK):
+            words = sb("picked_words%d" % c, [P, BANK], U32)
+            cols = slice(c * BANK // 16, (c + 1) * BANK // 16)
+            nc.vector.tensor_copy(words[:], word_table[:].bitcast(U32).indirect(offs_sb[:, cols]))
+            picked_words.append(words)
+
+        turn = [0]
+
+        def project(name, wq, t, on_vector):
+            rows = sb("%s%d" % (name, t), [P, S], F32)
+            codes, scales = wq
+            feats = slice(t * P, (t + 1) * P)
+            for c in range(S // BANK):
+                bank = banks[turn[0] % 4]
+                turn[0] = turn[0] + 1
+                cols = slice(c * BANK, (c + 1) * BANK)
+                nc.tensor.matmul_mx(
+                    out=bank[:],
+                    lhsT=codes[:, feats].bitcast(FP8X4),
+                    lhsT_scale=scales[:, feats],
+                    rhs=picked_words[c][:].bitcast(FP8X4),
+                    rhs_scale=picked_scales[:, cols],
+                    start=True,
+                    stop=True,
+                )
+                if on_vector:
+                    nc.vector.tensor_copy(rows[:, cols], bank[:])
+                else:
+                    nc.scalar.copy(rows[:, cols], bank[:])
+            return rows
+
+        y, e = {}, {}
+        y[0] = project("y", w1_q, 0, True)
+        w2_grouped = group_dealt("w2", w2_raw)
+        y[1] = project("y", w1_q, 1, False)
+
+        terms = {}
+
+        def look_up(name, t, lo, hi, rows, offsets, other, op):
+            if (name, t) not in terms:
+                terms[(name, t)] = sb("%s%d" % (name, t), [P, V], F32)
+            nc.vector.tensor_tensor(
+                terms[(name, t)][:, lo:hi], rows[:].indirect(offsets[:, lo // 16 : hi // 16]), other[:, lo:hi], op
+            )
+
+        def cy(t, lo=0, hi=V):
+            look_up("cy", t, lo, hi, y[t], right_sb, cw_sb[t], MULT)
+
+        def sy(t, lo=0, hi=V):
+            look_up("sy", t, lo, hi, y[t], right_sb, sw_sb[t], MULT)
+
+        def se(t, lo=0, hi=V):
+            look_up("se", t, lo, hi, e[t], right_sb, sw_sb[t], MULT)
+
+        def ce(t, lo=0, hi=V):
+            look_up("ce", t, lo, hi, e[t], right_sb, cw_sb[t], MULT)
+
+        def yl(t, lo=0, hi=V):
+            look_up("yl", t, lo, hi, y[t], left_sb, terms[("se", t)], SUB)
+
+        def el(t, lo=0, hi=V):
+            look_up("el", t, lo, hi, e[t], left_sb, terms[("sy", t)], ADD)
+
+        pairs = (("cy", "yl"), ("ce", "el"))
+
+        def add_turned(part, t, half):
+            bank = banks[4 + 2 * half + part]
+            for q in range(2):
+                cols = slice(half * HALF + q * P, half * HALF + (q + 1) * P)
+                place = (2 * q + t % 2) * P
+                for i, name in enumerate(pairs[part]):
+                    nc.tensor.matmul(
+                        bank[:, place : place + P],
+                        terms[(name, t)][:, cols],
+                        identity[:],
+                        start=(i == 0),
+                        stop=(i == 1),
+                        is_transpose=True,
+                    )
+
+        turned = {}
+
+        def round_turned(part, u, half):
+            tile = sb("turned%d%d%d" % (part, u, half), [P, 2 * P * 2], BF16)
+            nc.scalar.copy(
+                out=tile[:].rearrange("v (q p e) -> v q p e", q=2, e=2),
+                in_=banks[4 + 2 * half + part][:].rearrange("v (q e p) -> v q p e", q=2, e=2),
+            )
+            turned[(part, u, half)] = tile
+
+        def turn_back(part, half, on_vector):
+            bank = banks[part]
+            for u in range(2):
+                words = turned[(part, u, half)][:].bitcast(F32)
+                for q in range(2):
+                    place = (2 * u + q) * P
+                    nc.tensor.transpose(bank[:, place : place + P], words[:, q * P : (q + 1) * P], identity[:])
+            grouped = sb("z%d%d_bf16" % (part, half), [P, HALF * PACK], BF16)
+            dst = grouped[:].bitcast(F32).rearrange("p (v u) -> p v u", u=2)
+            src = bank[:].rearrange("p (u v) -> p v u", u=2)
+            if on_vector:
+                nc.vector.tensor_copy(dst, src)
+            else:
+                nc.scalar.copy(dst, src)
+            return grouped
+
+        cy(0)
+        sy(0)
+        w2_q = quantize("w2", w2_grouped[:])
+        e[0] = project("e", w2_q, 0, False)
+        e[1] = project("e", w2_q, 1, False)
+        for t in (2, 3):
+            y[t] = project("y", w1_q, t, False)
+            e[t] = project("e", w2_q, t, False)
+        w3_grouped = group_plain("w3", w3_raw)
+        w4_grouped = group_plain("w4", w4_raw)
+        cy(1)
+        sy(1)
+        for t in (0, 1):
+            se(t)
+            ce(t)
+            yl(t)
+            el(t)
+            for part in range(2):
+                for half in range(2):
+                    add_turned(part, t, half)
+        for half in range(2):
+            for part in range(2):
+                round_turned(part, 0, half)
+        w_last = (quantize("w3", w3_grouped[:]), quantize("w4", w4_grouped[:]))
+        se(2)
+        cy(2)
+        yl(2)
+        sy(2)
+        ce(2)
+        el(2)
+        for part in range(2):
+            for half in range(2):
+                add_turned(part, 2, half)
+
+        out_banks = ((2, 2, 3, 3), (4, 5, 6, 0))
+        out_rows = out.rearrange("(a p) v -> p a v", p=P)
+        for half in range(2):
+            lo, hi = half * HALF, (half + 1) * HALF
+            z_q = []
+            for part, steps in enumerate(((se, cy, yl), (sy, ce, el))):
+                for step in steps:
+                    step(3, lo, hi)
+                add_turned(part, 3, half)
+                round_turned(part, 1, half)
+                grouped = turn_back(part, half, half == 1 and part == 1)
+                z_q.append(quantize("z%d%d" % (part, half), grouped[:]))
+            order = [(a, part) for a in range(4) for part in range(2)]
+            if half == 1:
+                order = [(a, part) for part in range(2) for a in range(4)]
+            result = sb("result%d" % half, [P, 4, HALF], F32)
+            for a, part in order:
+                place = (a % 2) * HALF if half == 0 else 0
+                acc = banks[out_banks[half][a]][:, place : place + HALF]
+                feats = slice(a * P, (a + 1) * P)
+                nc.tensor.matmul_mx(
+                    out=acc,
+                    lhsT=w_last[part][0][:, feats].bitcast(FP8X4),
+                    lhsT_scale=w_last[part][1][:, feats],
+                    rhs=z_q[part][0][:].bitcast(FP8X4),
+                    rhs_scale=z_q[part][1][:],
+                    start=(part == 0),
+                    stop=(part == 1),
+                )
+                if part == 1 and half == 1:
+                    if a % 2 == 0:
+                        nc.vector.tensor_copy(result[:, a, :], acc)
+                    else:
+                        nc.scalar.copy(result[:, a, :], acc)
+                        nc.sync.dma_start(out=out_rows[:, a - 1 : a + 1, lo:hi], in_=result[:, a - 1 : a + 1, :])
+                if part == 1 and half == 0 and a % 2 == 1:
+                    nc.scalar.copy(
+                        result[:, a - 1 : a + 1, :].rearrange("p a v -> p (a v)"), banks[out_banks[half][a]][:]
+                    )
+                    nc.sync.dma_start(out=out_rows[:, a - 1 : a + 1, lo:hi], in_=result[:, a - 1 : a + 1, :])

@@ -11,8 +11,8 @@ U16 = mybir.dt.uint16
 U8 = mybir.dt.uint8
 FP8X4 = mybir.dt.float8_e4m3fn_x4
 MULT = mybir.AluOpType.mult
-ADD = mybir.AluOpType.add
 SUB = mybir.AluOpType.subtract
+COPY = mybir.ActivationFunctionType.Copy
 
 P = 128
 PACK = 4
@@ -48,24 +48,29 @@ def tile_picked_cbutter_none_p_kernel(
                 in_=x_scales[0, 4 * quad : 4 * quad + 4, :].bitcast(I32).unsqueeze(0).to_broadcast([8, 4, T // 4]),
             )
 
-        def load_weight(name, w):
-            raw = sb(name, [P, PACK, w.shape[1]], F32)
-            nc.sync.dma_start(out=raw[:], in_=w.rearrange("(p j) c -> p j c", j=PACK))
+        def load_rows(name, w, lo, hi):
+            raw = sb(name, [P, PACK, hi - lo], F32)
+            nc.sync.dma_start(out=raw[:], in_=w.rearrange("(p j) c -> p j c", j=PACK)[:, :, lo:hi])
             return raw
 
-        w1_raw = load_weight("w1_raw", w1)
-        nc.sync.dma_start(out=word_table[:], in_=x_words[0].rearrange("p n j -> p (n j)").bitcast(I32))
-        w2_raw = load_weight("w2_raw", w2)
-        nc.sync.dma_start(right_sb[:], right)
-        nc.sync.dma_start(left_sb[:], left)
         cw_sb, sw_sb = [], []
-        for first, count in ((0, 1), (1, 1), (2, 2)):
+
+        def load_twiddles(first, count):
             for name, src, tiles in (("cw", cw, cw_sb), ("sw", sw, sw_sb)):
                 rows = sb("%s%d" % (name, first), [P, count, V], F32)
                 nc.sync.dma_start(out=rows[:], in_=src.rearrange("(p t) v -> p t v", t=PACK)[:, first : first + count, :])
                 tiles.extend(rows[:, i, :] for i in range(count))
-        w3_raw = load_weight("w3_raw", w3)
-        w4_raw = load_weight("w4_raw", w4)
+
+        nc.sync.dma_start(out=word_table[:], in_=x_words[0].rearrange("p n j -> p (n j)").bitcast(I32))
+        w1_raw = [load_rows("w1_raw%d" % i, w1, i * H // 2, (i + 1) * H // 2) for i in range(2)]
+        w2_raw = [load_rows("w2_raw%d" % i, w2, i * H // 2, (i + 1) * H // 2) for i in range(2)]
+        nc.sync.dma_start(right_sb[:], right)
+        nc.sync.dma_start(left_sb[:], left)
+        load_twiddles(0, 1)
+        load_twiddles(1, 1)
+        load_twiddles(2, 2)
+        w3_raw = load_rows("w3_raw", w3, 0, N)
+        w4_raw = load_rows("w4_raw", w4, 0, N)
 
         identity = sb("identity", [P, P], F32)
         make_identity(nc, identity[:])
@@ -77,13 +82,12 @@ def tile_picked_cbutter_none_p_kernel(
             nc.vector.quantize_mx(out=codes[:].bitcast(FP8X4), scales=scales[:], in_=grouped)
             return codes, scales
 
-        def group_dealt(name, raw):
-            grouped = sb(name + "_bf16", [P, H * PACK], BF16)
-            nc.scalar.copy(
-                out=grouped[:].rearrange("p (t m j) -> p m j t", t=PACK, j=PACK),
-                in_=raw[:].rearrange("p j (m t) -> p m j t", t=PACK),
+        def deal(copy, grouped, raw, first):
+            count = raw.shape[2] // PACK
+            copy(
+                grouped[:].rearrange("p (t m j) -> p m j t", t=PACK, j=PACK)[:, first : first + count],
+                raw[:].rearrange("p j (m t) -> p m j t", t=PACK),
             )
-            return grouped
 
         def group_plain(name, raw):
             grouped = sb(name + "_bf16", [P, N * PACK], BF16)
@@ -95,7 +99,6 @@ def tile_picked_cbutter_none_p_kernel(
 
         picked_scales = sb("picked_scales", [P, S], U8)
         nc.vector.tensor_copy(picked_scales[:], scale_table[:].indirect(offs_sb[:]))
-        w1_q = quantize("w1", group_dealt("w1", w1_raw)[:])
         picked_words = []
         for c in range(S // BANK):
             words = sb("picked_words%d" % c, [P, BANK], U32)
@@ -103,177 +106,181 @@ def tile_picked_cbutter_none_p_kernel(
             nc.vector.tensor_copy(words[:], word_table[:].bitcast(U32).indirect(offs_sb[:, cols]))
             picked_words.append(words)
 
-        turn = [0]
+        w1_grouped = sb("w1_bf16", [P, H * PACK], BF16)
+        deal(nc.scalar.copy, w1_grouped, w1_raw[0], 0)
+        deal(nc.vector.tensor_copy, w1_grouped, w1_raw[1], P // 2)
+        w1_q = []
+        for first, count in ((0, 1), (1, 1), (2, 2)):
+            codes, scales = quantize("w1_%d" % first, w1_grouped[:, first * H : (first + count) * H])
+            w1_q.extend((codes[:, i * P : (i + 1) * P], scales[:, i * P : (i + 1) * P]) for i in range(count))
 
-        def project(name, wq, t, on_vector):
+        def negate(dst, src):
+            nc.scalar.activation(dst, src, COPY, scale=-1.0)
+
+        def negate_v(dst, src):
+            nc.vector.tensor_scalar(dst, src, -1.0, None, MULT)
+
+        def project(name, t, wq, bank_ids, copies):
             rows = sb("%s%d" % (name, t), [P, S], F32)
-            codes, scales = wq
-            feats = slice(t * P, (t + 1) * P)
             for c in range(S // BANK):
-                bank = banks[turn[0] % 4]
-                turn[0] = turn[0] + 1
+                bank = banks[bank_ids[c]]
                 cols = slice(c * BANK, (c + 1) * BANK)
                 nc.tensor.matmul_mx(
                     out=bank[:],
-                    lhsT=codes[:, feats].bitcast(FP8X4),
-                    lhsT_scale=scales[:, feats],
+                    lhsT=wq[0].bitcast(FP8X4),
+                    lhsT_scale=wq[1],
                     rhs=picked_words[c][:].bitcast(FP8X4),
                     rhs_scale=picked_scales[:, cols],
                     start=True,
                     stop=True,
                 )
-                if on_vector:
-                    nc.vector.tensor_copy(rows[:, cols], bank[:])
-                else:
-                    nc.scalar.copy(rows[:, cols], bank[:])
+                copies[c](rows[:, cols], bank[:])
             return rows
 
-        y, e = {}, {}
-        y[0] = project("y", w1_q, 0, True)
-        w2_grouped = group_dealt("w2", w2_raw)
-        y[1] = project("y", w1_q, 1, False)
+        plain = (nc.scalar.copy, nc.scalar.copy)
+        w2_grouped = sb("w2_bf16", [P, H * PACK], BF16)
+        for i in range(2):
+            deal(nc.scalar.copy, w2_grouped, w2_raw[i], i * P // 2)
+        y = [project("y", 0, w1_q[0], (0, 1), (nc.vector.tensor_copy, nc.vector.tensor_copy))]
+        y.append(project("y", 1, w1_q[1], (2, 3), plain))
+        y.append(project("y", 2, w1_q[2], (0, 1), plain))
+        y.append(project("y", 3, w1_q[3], (2, 3), plain))
 
-        terms = {}
-
-        def look_up(name, t, lo, hi, rows, offsets, other, op):
-            if (name, t) not in terms:
-                terms[(name, t)] = sb("%s%d" % (name, t), [P, V], F32)
-            nc.vector.tensor_tensor(
-                terms[(name, t)][:, lo:hi], rows[:].indirect(offsets[:, lo // 16 : hi // 16]), other[:, lo:hi], op
+        def add_turned(bank, t, term, start, stop):
+            nc.tensor.matmul(
+                bank[:, t * P : (t + 1) * P], term, identity[:], start=start, stop=stop, is_transpose=True
             )
 
-        def cy(t, lo=0, hi=V):
-            look_up("cy", t, lo, hi, y[t], right_sb, cw_sb[t], MULT)
-
-        def sy(t, lo=0, hi=V):
-            look_up("sy", t, lo, hi, y[t], right_sb, sw_sb[t], MULT)
-
-        def se(t, lo=0, hi=V):
-            look_up("se", t, lo, hi, e[t], right_sb, sw_sb[t], MULT)
-
-        def ce(t, lo=0, hi=V):
-            look_up("ce", t, lo, hi, e[t], right_sb, cw_sb[t], MULT)
-
-        def yl(t, lo=0, hi=V):
-            look_up("yl", t, lo, hi, y[t], left_sb, terms[("se", t)], SUB)
-
-        def el(t, lo=0, hi=V):
-            look_up("el", t, lo, hi, e[t], left_sb, terms[("sy", t)], ADD)
-
-        pairs = (("cy", "yl"), ("ce", "el"))
-
-        def add_turned(part, t, half):
-            bank = banks[4 + 2 * half + part]
-            for q in range(2):
-                cols = slice(half * HALF + q * P, half * HALF + (q + 1) * P)
-                place = (2 * q + t % 2) * P
-                for i, name in enumerate(pairs[part]):
-                    nc.tensor.matmul(
-                        bank[:, place : place + P],
-                        terms[(name, t)][:, cols],
-                        identity[:],
-                        start=(i == 0),
-                        stop=(i == 1),
-                        is_transpose=True,
+        sy = []
+        for t in range(PACK):
+            yr = sb("yr%d" % t, [P, V], F32)
+            yl = sb("yl%d" % t, [P, V], F32)
+            cy = sb("cy%d" % t, [P, V], F32)
+            sy.append(sb("sy%d" % t, [P, V], F32))
+            nc.vector.tensor_copy(yr[:], y[t][:].indirect(right_sb[:]))
+            if t == 0:
+                codes, scales = quantize("w2", w2_grouped[:])
+            nc.vector.tensor_copy(yl[:], y[t][:].indirect(left_sb[:]))
+            nc.gpsimd.tensor_tensor(cy[:], yr[:], cw_sb[t], MULT)
+            nc.gpsimd.tensor_tensor(sy[t][:], yr[:], sw_sb[t], MULT)
+            if t == 0:
+                e = [
+                    project(
+                        "e", s, (codes[:, s * P : (s + 1) * P], scales[:, s * P : (s + 1) * P]),
+                        (0, 1) if s % 2 == 0 else (2, 3), (negate, negate) if s < 3 else (negate_v, negate_v),
                     )
+                    for s in range(PACK)
+                ]
+            for q in range(4):
+                add_turned(banks[4 + q], t, yl[:, q * P : (q + 1) * P], t == 0, False)
+            for q in range(4):
+                add_turned(banks[4 + q], t, cy[:, q * P : (q + 1) * P], False, False)
 
-        turned = {}
-
-        def round_turned(part, u, half):
-            tile = sb("turned%d%d%d" % (part, u, half), [P, 2 * P * 2], BF16)
-            nc.scalar.copy(
-                out=tile[:].rearrange("v (q p e) -> v q p e", q=2, e=2),
-                in_=banks[4 + 2 * half + part][:].rearrange("v (q e p) -> v q p e", q=2, e=2),
-            )
-            turned[(part, u, half)] = tile
-
-        def turn_back(part, half, on_vector):
-            bank = banks[part]
-            for u in range(2):
-                words = turned[(part, u, half)][:].bitcast(F32)
-                for q in range(2):
-                    place = (2 * u + q) * P
-                    nc.tensor.transpose(bank[:, place : place + P], words[:, q * P : (q + 1) * P], identity[:])
-            grouped = sb("z%d%d_bf16" % (part, half), [P, HALF * PACK], BF16)
-            dst = grouped[:].bitcast(F32).rearrange("p (v u) -> p v u", u=2)
-            src = bank[:].rearrange("p (u v) -> p v u", u=2)
-            if on_vector:
-                nc.vector.tensor_copy(dst, src)
-            else:
-                nc.scalar.copy(dst, src)
-            return grouped
-
-        cy(0)
-        sy(0)
-        w2_q = quantize("w2", w2_grouped[:])
-        e[0] = project("e", w2_q, 0, False)
-        e[1] = project("e", w2_q, 1, False)
-        for t in (2, 3):
-            y[t] = project("y", w1_q, t, False)
-            e[t] = project("e", w2_q, t, False)
         w3_grouped = group_plain("w3", w3_raw)
         w4_grouped = group_plain("w4", w4_raw)
-        cy(1)
-        sy(1)
-        for t in (0, 1):
-            se(t)
-            ce(t)
-            yl(t)
-            el(t)
-            for part in range(2):
-                for half in range(2):
-                    add_turned(part, t, half)
-        for half in range(2):
-            for part in range(2):
-                round_turned(part, 0, half)
-        w_last = (quantize("w3", w3_grouped[:]), quantize("w4", w4_grouped[:]))
-        se(2)
-        cy(2)
-        yl(2)
-        sy(2)
-        ce(2)
-        el(2)
-        for part in range(2):
-            for half in range(2):
-                add_turned(part, 2, half)
 
-        out_banks = ((2, 2, 3, 3), (4, 5, 6, 0))
-        out_rows = out.rearrange("(a p) v -> p a v", p=P)
-        for half in range(2):
-            lo, hi = half * HALF, (half + 1) * HALF
-            z_q = []
-            for part, steps in enumerate(((se, cy, yl), (sy, ce, el))):
-                for step in steps:
-                    step(3, lo, hi)
-                add_turned(part, 3, half)
-                round_turned(part, 1, half)
-                grouped = turn_back(part, half, half == 1 and part == 1)
-                z_q.append(quantize("z%d%d" % (part, half), grouped[:]))
-            order = [(a, part) for a in range(4) for part in range(2)]
-            if half == 1:
-                order = [(a, part) for part in range(2) for a in range(4)]
-            result = sb("result%d" % half, [P, 4, HALF], F32)
-            for a, part in order:
-                place = (a % 2) * HALF if half == 0 else 0
-                acc = banks[out_banks[half][a]][:, place : place + HALF]
-                feats = slice(a * P, (a + 1) * P)
-                nc.tensor.matmul_mx(
-                    out=acc,
-                    lhsT=w_last[part][0][:, feats].bitcast(FP8X4),
-                    lhsT_scale=w_last[part][1][:, feats],
-                    rhs=z_q[part][0][:].bitcast(FP8X4),
-                    rhs_scale=z_q[part][1][:],
-                    start=(part == 0),
-                    stop=(part == 1),
+        def new_terms(label, shape, tag):
+            return keep.tile(shape, F32, name=label, tag=tag, align_bytes=64)
+
+        def look_up(term, t, lo, hi, offsets, other, op):
+            nc.vector.tensor_tensor(term, e[t][:].indirect(offsets[:, lo // 16 : hi // 16]), other[:, lo:hi], op)
+
+        def left_term(t, half, tag):
+            lo = half * HALF
+            term = new_terms("el%d%d" % (t, half), [P, HALF], tag)
+            look_up(term[:], t, lo, lo + HALF, left_sb, sy[t], SUB)
+            for i in range(2):
+                add_turned(banks[i], t, term[:, i * P : (i + 1) * P], t == 0, False)
+
+        def right_term(term, part, t, q, count):
+            look_up(term, t, q * P, (q + count) * P, right_sb, (sw_sb, cw_sb)[part][t], MULT)
+            for i in range(count):
+                bank = banks[4 + q + i] if part == 0 else banks[(q + i) % 2]
+                add_turned(bank, t, term[:, i * P : (i + 1) * P], False, t == PACK - 1)
+
+        def right_quarter(part, q, tag):
+            terms = new_terms("er%d%d" % (part, q), [P, PACK, P], tag)
+            for t in range(PACK):
+                right_term(terms[:, t, :], part, t, q, 1)
+
+        def regroup(part, q, count, last_copy):
+            back = banks[2 + part]
+            for i in range(count):
+                label = "turned%d%d" % (part, q + i)
+                turned = keep.tile([P, H], BF16, name=label, tag=label, align_bytes=64)
+                bank = banks[4 + q + i] if part == 0 else banks[(q + i) % 2]
+                (nc.scalar.copy, negate)[part](
+                    turned[:].rearrange("v (u p e) -> v u p e", u=2, e=2),
+                    bank[:].rearrange("v (u e p) -> v u p e", u=2, e=2),
                 )
-                if part == 1 and half == 1:
-                    if a % 2 == 0:
-                        nc.vector.tensor_copy(result[:, a, :], acc)
-                    else:
-                        nc.scalar.copy(result[:, a, :], acc)
-                        nc.sync.dma_start(out=out_rows[:, a - 1 : a + 1, lo:hi], in_=result[:, a - 1 : a + 1, :])
-                if part == 1 and half == 0 and a % 2 == 1:
-                    nc.scalar.copy(
-                        result[:, a - 1 : a + 1, :].rearrange("p a v -> p (a v)"), banks[out_banks[half][a]][:]
-                    )
-                    nc.sync.dma_start(out=out_rows[:, a - 1 : a + 1, lo:hi], in_=result[:, a - 1 : a + 1, :])
+                words = turned[:].bitcast(F32)
+                for u in range(2):
+                    place = (u * count + i) * P
+                    nc.tensor.transpose(back[:, place : place + P], words[:, u * P : (u + 1) * P], identity[:])
+            label = "z%d%d_bf16" % (part, q)
+            grouped = keep.tile([P, count * P * PACK], BF16, name=label, tag=label, align_bytes=64)
+            last_copy(
+                grouped[:].bitcast(F32).rearrange("p (v u) -> p v u", u=2),
+                back[:, 0 : 2 * count * P].rearrange("p (u v) -> p v u", u=2),
+            )
+            return grouped
+
+        out_rows = out.rearrange("(a p) v -> p a v", p=P)
+
+        def last_pass(acc, a, part, z_q):
+            feats = slice(a * P, (a + 1) * P)
+            nc.tensor.matmul_mx(
+                out=acc,
+                lhsT=w_last[part][0][:, feats].bitcast(FP8X4),
+                lhsT_scale=w_last[part][1][:, feats],
+                rhs=z_q[0][:].bitcast(FP8X4),
+                rhs_scale=z_q[1][:],
+                start=(part == 0),
+                stop=(part == 1),
+            )
+
+        for t in range(PACK):
+            left_term(t, 0, "a%d0" % t)
+            for part in range(2):
+                label = "a%d%d" % (t, part + 1)
+                right_term(new_terms(label, [P, HALF], label)[:], part, t, 0, 2)
+        grouped = [regroup(part, 0, 2, nc.scalar.copy) for part in range(2)]
+        w_last = (quantize("w3", w3_grouped[:]), quantize("w4", w4_grouped[:]))
+        for t in range(PACK):
+            left_term(t, 1, "a3%d" % t)
+        right_quarter(0, 2, "turned01")
+        z_q = [quantize("z%d0" % part, grouped[part][:]) for part in range(2)]
+        result = sb("result0", [P, 4, HALF], F32)
+        for a in range(4):
+            bank = banks[4 + a // 2]
+            for part in range(2):
+                last_pass(bank[:, (a % 2) * HALF : (a % 2 + 1) * HALF], a, part, z_q[part])
+            if a % 2 == 1:
+                nc.scalar.copy(result[:, a - 1 : a + 1, :].rearrange("p a v -> p (a v)"), bank[:])
+        nc.sync.dma_start(out=out_rows[:, :, 0:HALF], in_=result[:])
+
+        grouped = [regroup(0, 2, 1, nc.scalar.copy)]
+        right_quarter(1, 2, "z00_bf16")
+        grouped.append(regroup(1, 2, 1, nc.scalar.copy))
+        right_quarter(0, 3, "z10_bf16")
+        z_q = [quantize("z02", grouped[0][:])]
+        last_grouped = regroup(0, 3, 1, nc.scalar.copy)
+        right_quarter(1, 3, "z02_bf16")
+        z_q.append(quantize("z12", grouped[1][:]))
+        result = sb("result2", [P, 4, P], F32)
+        for a in range(4):
+            for part in range(2):
+                last_pass(banks[6][:, a * P : (a + 1) * P], a, part, z_q[part])
+        nc.scalar.copy(result[:].rearrange("p a v -> p (a v)"), banks[6][:])
+        nc.sync.dma_start(out=out_rows[:, :, 2 * P : 3 * P], in_=result[:])
+
+        accs = [banks[b][:, 0:P] for b in (4, 5, 7, 2)]
+        z_real = quantize("z03", last_grouped[:])
+        for a in range(4):
+            last_pass(accs[a], a, 0, z_real)
+        z_imag = quantize("z13", regroup(1, 3, 1, nc.vector.tensor_copy)[:])
+        result = sb("result3", [P, 4, P], F32)
+        for a in range(4):
+            last_pass(accs[a], a, 1, z_imag)
+            (nc.vector.tensor_copy, nc.scalar.copy)[a % 2](result[:, a, :], accs[a])
+        nc.sync.dma_start(out=out_rows[:, :, 3 * P : 4 * P], in_=result[:])

@@ -11,6 +11,7 @@ U16 = mybir.dt.uint16
 U8 = mybir.dt.uint8
 FP8X4 = mybir.dt.float8_e4m3fn_x4
 MULT = mybir.AluOpType.mult
+ADD = mybir.AluOpType.add
 SUB = mybir.AluOpType.subtract
 COPY = mybir.ActivationFunctionType.Copy
 
@@ -57,7 +58,8 @@ def tile_picked_cbutter_none_p_kernel(
 
         def load_twiddles(first, count):
             for name, src, tiles in (("cw", cw, cw_sb), ("sw", sw, sw_sb)):
-                rows = sb("%s%d" % (name, first), [P, count, V], F32)
+                label = "%s%d" % (name, first)
+                rows = keep.tile([P, count, V], F32, name=label, tag=label, align_bytes=64)
                 nc.sync.dma_start(out=rows[:], in_=src.rearrange("(p t) v -> p t v", t=PACK)[:, first : first + count, :])
                 tiles.extend(rows[:, i, :] for i in range(count))
 
@@ -68,16 +70,17 @@ def tile_picked_cbutter_none_p_kernel(
         nc.sync.dma_start(left_sb[:], left)
         load_twiddles(0, 1)
         load_twiddles(1, 1)
-        load_twiddles(2, 2)
+        load_twiddles(2, 1)
+        load_twiddles(3, 1)
         w3_raw = load_rows("w3_raw", w3, 0, N)
         w4_raw = load_rows("w4_raw", w4, 0, N)
 
         identity = sb("identity", [P, P], F32)
         make_identity(nc, identity[:])
 
-        def quantize(name, grouped):
+        def quantize(name, grouped, tag=None):
             width = grouped.shape[1] // PACK
-            codes = sb(name + "_codes", [P, width], U32)
+            codes = keep.tile([P, width], U32, name=name + "_codes", tag=tag or name + "_codes", align_bytes=64)
             scales = sb(name + "_scales", [P, width], U8)
             nc.vector.quantize_mx(out=codes[:].bitcast(FP8X4), scales=scales[:], in_=grouped)
             return codes, scales
@@ -89,13 +92,11 @@ def tile_picked_cbutter_none_p_kernel(
                 raw[:].rearrange("p j (m t) -> p m j t", t=PACK),
             )
 
-        def group_plain(name, raw):
-            grouped = sb(name + "_bf16", [P, N * PACK], BF16)
-            nc.scalar.copy(
-                out=grouped[:].rearrange("p (c i j) -> p c j i", i=4, j=PACK),
-                in_=raw[:].rearrange("p j (c i) -> p c j i", i=4),
+        def weave(copy, grouped, rows):
+            copy(
+                grouped.rearrange("p (c i j) -> p c j i", i=4, j=PACK),
+                rows.rearrange("p j (c i) -> p c j i", i=4),
             )
-            return grouped
 
         picked_scales = sb("picked_scales", [P, S], U8)
         nc.vector.tensor_copy(picked_scales[:], scale_table[:].indirect(offs_sb[:]))
@@ -120,10 +121,10 @@ def tile_picked_cbutter_none_p_kernel(
         def negate_v(dst, src):
             nc.vector.tensor_scalar(dst, src, -1.0, None, MULT)
 
-        def project(name, t, wq, bank_ids, copies):
+        def project(name, t, wq, first_bank, copy):
             rows = sb("%s%d" % (name, t), [P, S], F32)
             for c in range(S // BANK):
-                bank = banks[bank_ids[c]]
+                bank = banks[first_bank + c]
                 cols = slice(c * BANK, (c + 1) * BANK)
                 nc.tensor.matmul_mx(
                     out=bank[:],
@@ -134,153 +135,156 @@ def tile_picked_cbutter_none_p_kernel(
                     start=True,
                     stop=True,
                 )
-                copies[c](rows[:, cols], bank[:])
+                copy(rows[:, cols], bank[:])
             return rows
 
-        plain = (nc.scalar.copy, nc.scalar.copy)
         w2_grouped = sb("w2_bf16", [P, H * PACK], BF16)
         for i in range(2):
             deal(nc.scalar.copy, w2_grouped, w2_raw[i], i * P // 2)
-        y = [project("y", 0, w1_q[0], (0, 1), (nc.vector.tensor_copy, nc.vector.tensor_copy))]
-        y.append(project("y", 1, w1_q[1], (2, 3), plain))
-        y.append(project("y", 2, w1_q[2], (0, 1), plain))
-        y.append(project("y", 3, w1_q[3], (2, 3), plain))
+        y, e = {}, {}
+        y[0] = project("y", 0, w1_q[0], 0, negate_v)
+        y[1] = project("y", 1, w1_q[1], 2, negate)
+        codes, scales = quantize("w2", w2_grouped[:])
+        w2_q = [(codes[:, s * P : (s + 1) * P], scales[:, s * P : (s + 1) * P]) for s in range(PACK)]
+        e[0] = project("e", 0, w2_q[0], 4, nc.scalar.copy)
+        y[2] = project("y", 2, w1_q[2], 6, negate)
+        e[1] = project("e", 1, w2_q[1], 0, nc.scalar.copy)
+        e[2] = project("e", 2, w2_q[2], 2, nc.scalar.copy)
+        y[3] = project("y", 3, w1_q[3], 4, negate)
+        e[3] = project("e", 3, w2_q[3], 6, nc.scalar.copy)
+        w34_grouped = sb("w34_bf16", [P, 2 * N * PACK], BF16)
+        for part, raw in enumerate((w3_raw, w4_raw)):
+            weave(nc.scalar.copy, w34_grouped[:, part * N * PACK : (part + 1) * N * PACK], raw[:])
 
-        def add_turned(bank, t, term, start, stop):
-            nc.tensor.matmul(
-                bank[:, t * P : (t + 1) * P], term, identity[:], start=start, stop=stop, is_transpose=True
-            )
-
-        sy = []
-        for t in range(PACK):
-            yr = sb("yr%d" % t, [P, V], F32)
-            yl = sb("yl%d" % t, [P, V], F32)
-            cy = sb("cy%d" % t, [P, V], F32)
-            sy.append(sb("sy%d" % t, [P, V], F32))
-            nc.vector.tensor_copy(yr[:], y[t][:].indirect(right_sb[:]))
-            if t == 0:
-                codes, scales = quantize("w2", w2_grouped[:])
-            nc.vector.tensor_copy(yl[:], y[t][:].indirect(left_sb[:]))
-            nc.gpsimd.tensor_tensor(cy[:], yr[:], cw_sb[t], MULT)
-            nc.gpsimd.tensor_tensor(sy[t][:], yr[:], sw_sb[t], MULT)
-            if t == 0:
-                e = [
-                    project(
-                        "e", s, (codes[:, s * P : (s + 1) * P], scales[:, s * P : (s + 1) * P]),
-                        (0, 1) if s % 2 == 0 else (2, 3), (negate, negate) if s < 3 else (negate_v, negate_v),
-                    )
-                    for s in range(PACK)
-                ]
+        def add_turned(t, term, start=False, stop=False):
             for q in range(4):
-                add_turned(banks[4 + q], t, yl[:, q * P : (q + 1) * P], t == 0, False)
-            for q in range(4):
-                add_turned(banks[4 + q], t, cy[:, q * P : (q + 1) * P], False, False)
+                nc.tensor.matmul(
+                    banks[4 + q][:, t * P : (t + 1) * P], term[:, q * P : (q + 1) * P], identity[:],
+                    start=start, stop=stop, is_transpose=True,
+                )
 
-        w3_grouped = group_plain("w3", w3_raw)
-        w4_grouped = group_plain("w4", w4_raw)
+        def fetch(label, rows, offsets):
+            term = keep.tile([P, V], F32, name=label, tag=label, align_bytes=64)
+            nc.vector.tensor_copy(term[:], rows[:].indirect(offsets[:]))
+            return term
 
-        def new_terms(label, shape, tag):
-            return keep.tile(shape, F32, name=label, tag=tag, align_bytes=64)
+        sy = sb("sy", [P, PACK - 1, V], F32)
+        ce = sb("ce", [P, PACK - 2, V], F32)
+        yr, er = {}, {}
 
-        def look_up(term, t, lo, hi, offsets, other, op):
-            nc.vector.tensor_tensor(term, e[t][:].indirect(offsets[:, lo // 16 : hi // 16]), other[:, lo:hi], op)
+        def y_terms(t):
+            yr[t] = fetch("yr%d" % t, y[t], right_sb)
+            yl = fetch("yl%d" % t, y[t], left_sb)
+            add_turned(t, yl, start=(t == 0))
+            if t < PACK - 1:
+                cy = sb("cy%d" % t, [P, V], F32)
+                nc.gpsimd.tensor_tensor(cy[:], yr[t][:], cw_sb[t], MULT)
+                nc.gpsimd.tensor_tensor(sy[:, t, :], yr[t][:], sw_sb[t], MULT)
+                add_turned(t, cy)
 
-        def left_term(t, half, tag):
-            lo = half * HALF
-            term = new_terms("el%d%d" % (t, half), [P, HALF], tag)
-            look_up(term[:], t, lo, lo + HALF, left_sb, sy[t], SUB)
+        def e_terms(t):
+            er[t] = fetch("er%d" % t, e[t], right_sb)
+            if t < PACK - 2:
+                se = sb("se%d" % t, [P, V], F32)
+                nc.gpsimd.tensor_tensor(se[:], er[t][:], sw_sb[t], MULT)
+                nc.gpsimd.tensor_tensor(ce[:, t, :], er[t][:], cw_sb[t], MULT)
+                add_turned(t, se)
+
+        y_terms(0)
+        y_terms(1)
+        e_terms(0)
+        y_terms(2)
+        e_terms(1)
+        e_terms(2)
+        y_terms(3)
+        e_terms(3)
+
+        last = keep.tile([P, 6, V], F32, name="last", tag="er1", align_bytes=64)
+        for i, (term, factor) in enumerate(
+            ((er[2], sw_sb[2]), (yr[3], cw_sb[3]), (er[3], sw_sb[3]), (er[2], cw_sb[2]), (er[3], cw_sb[3]), (yr[3], sw_sb[3]))
+        ):
+            nc.vector.tensor_tensor(last[:, i, :], term[:], factor, MULT)
+            if i < 3:
+                add_turned((2, 3, 3)[i], last[:, i, :], stop=(i == 2))
+
+        z_grouped = []
+        for half in range(2):
+            back = banks[half]
             for i in range(2):
-                add_turned(banks[i], t, term[:, i * P : (i + 1) * P], t == 0, False)
-
-        def right_term(term, part, t, q, count):
-            look_up(term, t, q * P, (q + count) * P, right_sb, (sw_sb, cw_sb)[part][t], MULT)
-            for i in range(count):
-                bank = banks[4 + q + i] if part == 0 else banks[(q + i) % 2]
-                add_turned(bank, t, term[:, i * P : (i + 1) * P], False, t == PACK - 1)
-
-        def right_quarter(part, q, tag):
-            terms = new_terms("er%d%d" % (part, q), [P, PACK, P], tag)
-            for t in range(PACK):
-                right_term(terms[:, t, :], part, t, q, 1)
-
-        def regroup(part, q, count, last_copy):
-            back = banks[2 + part]
-            for i in range(count):
-                label = "turned%d%d" % (part, q + i)
-                turned = keep.tile([P, H], BF16, name=label, tag=label, align_bytes=64)
-                bank = banks[4 + q + i] if part == 0 else banks[(q + i) % 2]
-                (nc.scalar.copy, negate)[part](
+                q = 2 * half + i
+                turned = sb("turned%d" % q, [P, H], BF16)
+                negate(
                     turned[:].rearrange("v (u p e) -> v u p e", u=2, e=2),
-                    bank[:].rearrange("v (u e p) -> v u p e", u=2, e=2),
+                    banks[4 + q][:].rearrange("v (u e p) -> v u p e", u=2, e=2),
                 )
                 words = turned[:].bitcast(F32)
                 for u in range(2):
-                    place = (u * count + i) * P
+                    place = (u * 2 + i) * P
                     nc.tensor.transpose(back[:, place : place + P], words[:, u * P : (u + 1) * P], identity[:])
-            label = "z%d%d_bf16" % (part, q)
-            grouped = keep.tile([P, count * P * PACK], BF16, name=label, tag=label, align_bytes=64)
-            last_copy(
+            grouped = sb("z%d_bf16" % half, [P, HALF * PACK], BF16)
+            nc.scalar.copy(
                 grouped[:].bitcast(F32).rearrange("p (v u) -> p v u", u=2),
-                back[:, 0 : 2 * count * P].rearrange("p (u v) -> p v u", u=2),
+                back[:].rearrange("p (u v) -> p v u", u=2),
             )
-            return grouped
+            z_grouped.append(grouped)
+
+        def mix(half):
+            cols = slice(half * HALF, (half + 1) * HALF)
+            mixed = sb("mixed%d" % half, [P, PACK, HALF], F32)
+            nc.vector.tensor_tensor(mixed[:, 0:2, :], ce[:, :, cols], sy[:, 0:2, cols], SUB)
+            nc.vector.tensor_tensor(mixed[:, 2, :], last[:, 3, cols], sy[:, 2, cols], SUB)
+            nc.vector.tensor_tensor(mixed[:, 3, :], last[:, 4, cols], last[:, 5, cols], SUB)
+            return mixed
+
+        def imag_rows(half, mixed, tag):
+            rows = keep.tile([P, PACK, HALF], F32, name="z2_rows%d" % half, tag=tag, align_bytes=64)
+            cols = slice(half * HALF // 16, (half + 1) * HALF // 16)
+            for t in range(PACK):
+                nc.vector.tensor_tensor(rows[:, t, :], e[t][:].indirect(left_sb[:, cols]), mixed[:, t, :], ADD)
+            return rows
 
         out_rows = out.rearrange("(a p) v -> p a v", p=P)
 
         def last_pass(acc, a, part, z_q):
-            feats = slice(a * P, (a + 1) * P)
+            feats = slice(part * N + a * P, part * N + (a + 1) * P)
             nc.tensor.matmul_mx(
                 out=acc,
-                lhsT=w_last[part][0][:, feats].bitcast(FP8X4),
-                lhsT_scale=w_last[part][1][:, feats],
+                lhsT=w34_q[0][:, feats].bitcast(FP8X4),
+                lhsT_scale=w34_q[1][:, feats],
                 rhs=z_q[0][:].bitcast(FP8X4),
                 rhs_scale=z_q[1][:],
                 start=(part == 0),
                 stop=(part == 1),
             )
 
-        for t in range(PACK):
-            left_term(t, 0, "a%d0" % t)
-            for part in range(2):
-                label = "a%d%d" % (t, part + 1)
-                right_term(new_terms(label, [P, HALF], label)[:], part, t, 0, 2)
-        grouped = [regroup(part, 0, 2, nc.scalar.copy) for part in range(2)]
-        w_last = (quantize("w3", w3_grouped[:]), quantize("w4", w4_grouped[:]))
-        for t in range(PACK):
-            left_term(t, 1, "a3%d" % t)
-        right_quarter(0, 2, "turned01")
-        z_q = [quantize("z%d0" % part, grouped[part][:]) for part in range(2)]
+        mixed = mix(0)
+        w34_q = quantize("w34", w34_grouped[:], "cw1")
+        rows = imag_rows(0, mixed, "z2_rows0")
+        z2_grouped = keep.tile([P, HALF * PACK], BF16, name="z2_bf16", tag="z2_bf16", align_bytes=64)
+        weave(nc.scalar.copy, z2_grouped[:], rows[:])
+        mixed = mix(1)
+        z_q = [quantize("z%d" % half, z_grouped[half][:]) for half in range(2)]
+        z2_q = quantize("z20", z2_grouped[:])
         result = sb("result0", [P, 4, HALF], F32)
         for a in range(4):
-            bank = banks[4 + a // 2]
-            for part in range(2):
-                last_pass(bank[:, (a % 2) * HALF : (a % 2 + 1) * HALF], a, part, z_q[part])
+            bank = banks[2 + a // 2]
+            acc = bank[:, (a % 2) * HALF : (a % 2 + 1) * HALF]
+            last_pass(acc, a, 0, z_q[0])
+            last_pass(acc, a, 1, z2_q)
             if a % 2 == 1:
                 nc.scalar.copy(result[:, a - 1 : a + 1, :].rearrange("p a v -> p (a v)"), bank[:])
         nc.sync.dma_start(out=out_rows[:, :, 0:HALF], in_=result[:])
 
-        grouped = [regroup(0, 2, 1, nc.scalar.copy)]
-        right_quarter(1, 2, "z00_bf16")
-        grouped.append(regroup(1, 2, 1, nc.scalar.copy))
-        right_quarter(0, 3, "z10_bf16")
-        z_q = [quantize("z02", grouped[0][:])]
-        last_grouped = regroup(0, 3, 1, nc.scalar.copy)
-        right_quarter(1, 3, "z02_bf16")
-        z_q.append(quantize("z12", grouped[1][:]))
-        result = sb("result2", [P, 4, P], F32)
+        accs = [banks[4 + a][:, 0:HALF] for a in range(4)]
         for a in range(4):
-            for part in range(2):
-                last_pass(banks[6][:, a * P : (a + 1) * P], a, part, z_q[part])
-        nc.scalar.copy(result[:].rearrange("p a v -> p (a v)"), banks[6][:])
-        nc.sync.dma_start(out=out_rows[:, :, 2 * P : 3 * P], in_=result[:])
-
-        accs = [banks[b][:, 0:P] for b in (4, 5, 7, 2)]
-        z_real = quantize("z03", last_grouped[:])
+            last_pass(accs[a], a, 0, z_q[1])
+        rows = imag_rows(1, mixed, "z2_bf16")
+        z2_grouped = sb("z21_bf16", [P, HALF * PACK], BF16)
+        weave(nc.vector.tensor_copy, z2_grouped[:], rows[:])
+        z2_q = quantize("z21", z2_grouped[:])
+        result = sb("result1", [P, 4, HALF], F32)
         for a in range(4):
-            last_pass(accs[a], a, 0, z_real)
-        z_imag = quantize("z13", regroup(1, 3, 1, nc.vector.tensor_copy)[:])
-        result = sb("result3", [P, 4, P], F32)
-        for a in range(4):
-            last_pass(accs[a], a, 1, z_imag)
+            last_pass(accs[a], a, 1, z2_q)
             (nc.vector.tensor_copy, nc.scalar.copy)[a % 2](result[:, a, :], accs[a])
-        nc.sync.dma_start(out=out_rows[:, :, 3 * P : 4 * P], in_=result[:])
+            if a % 2 == 1:
+                nc.sync.dma_start(out=out_rows[:, a - 1 : a + 1, HALF:V], in_=result[:, a - 1 : a + 1, :])

@@ -54,24 +54,23 @@ def tile_picked_cbutter_none_p_kernel(
             nc.sync.dma_start(out=raw[:], in_=w.rearrange("(p j) c -> p j c", j=PACK)[:, :, lo:hi])
             return raw
 
-        cw_sb, sw_sb = [], []
-
         def load_twiddles(first, count):
-            for name, src, tiles in (("cw", cw, cw_sb), ("sw", sw, sw_sb)):
-                label = "%s%d" % (name, first)
-                rows = keep.tile([P, count, V], F32, name=label, tag=label, align_bytes=64)
+            tiles = []
+            for name, src in (("cw", cw), ("sw", sw)):
+                rows = sb("%s%d" % (name, first), [P, count, V], F32)
                 nc.sync.dma_start(out=rows[:], in_=src.rearrange("(p t) v -> p t v", t=PACK)[:, first : first + count, :])
-                tiles.extend(rows[:, i, :] for i in range(count))
+                tiles.append(rows)
+            return tiles
 
         nc.sync.dma_start(out=word_table[:], in_=x_words[0].rearrange("p n j -> p (n j)").bitcast(I32))
         w1_raw = [load_rows("w1_raw%d" % i, w1, i * H // 2, (i + 1) * H // 2) for i in range(2)]
         w2_raw = [load_rows("w2_raw%d" % i, w2, i * H // 2, (i + 1) * H // 2) for i in range(2)]
         nc.sync.dma_start(right_sb[:], right)
         nc.sync.dma_start(left_sb[:], left)
-        load_twiddles(0, 1)
-        load_twiddles(1, 1)
-        load_twiddles(2, 1)
-        load_twiddles(3, 1)
+        cw_first, sw_first = load_twiddles(0, 1)
+        cw_rest, sw_rest = load_twiddles(1, PACK - 1)
+        cw_sb = [cw_first[:, 0, :]] + [cw_rest[:, i, :] for i in range(PACK - 1)]
+        sw_sb = [sw_first[:, 0, :]] + [sw_rest[:, i, :] for i in range(PACK - 1)]
         w3_raw = load_rows("w3_raw", w3, 0, N)
         w4_raw = load_rows("w4_raw", w4, 0, N)
 
@@ -118,9 +117,6 @@ def tile_picked_cbutter_none_p_kernel(
         def negate(dst, src):
             nc.scalar.activation(dst, src, COPY, scale=-1.0)
 
-        def negate_v(dst, src):
-            nc.vector.tensor_scalar(dst, src, -1.0, None, MULT)
-
         def project(name, t, wq, first_bank, copy):
             rows = sb("%s%d" % (name, t), [P, S], F32)
             for c in range(S // BANK):
@@ -139,18 +135,18 @@ def tile_picked_cbutter_none_p_kernel(
             return rows
 
         w2_grouped = sb("w2_bf16", [P, H * PACK], BF16)
-        for i in range(2):
-            deal(nc.scalar.copy, w2_grouped, w2_raw[i], i * P // 2)
+        deal(nc.scalar.copy, w2_grouped, w2_raw[0], 0)
+        deal(nc.vector.tensor_copy, w2_grouped, w2_raw[1], P // 2)
         y, e = {}, {}
-        y[0] = project("y", 0, w1_q[0], 0, negate_v)
+        y[0] = project("y", 0, w1_q[0], 0, negate)
         y[1] = project("y", 1, w1_q[1], 2, negate)
         codes, scales = quantize("w2", w2_grouped[:])
         w2_q = [(codes[:, s * P : (s + 1) * P], scales[:, s * P : (s + 1) * P]) for s in range(PACK)]
         e[0] = project("e", 0, w2_q[0], 4, nc.scalar.copy)
         y[2] = project("y", 2, w1_q[2], 6, negate)
-        e[1] = project("e", 1, w2_q[1], 0, nc.scalar.copy)
-        e[2] = project("e", 2, w2_q[2], 2, nc.scalar.copy)
-        y[3] = project("y", 3, w1_q[3], 4, negate)
+        y[3] = project("y", 3, w1_q[3], 0, negate)
+        e[1] = project("e", 1, w2_q[1], 2, nc.scalar.copy)
+        e[2] = project("e", 2, w2_q[2], 4, nc.scalar.copy)
         e[3] = project("e", 3, w2_q[3], 6, nc.scalar.copy)
         w34_grouped = sb("w34_bf16", [P, 2 * N * PACK], BF16)
         for part, raw in enumerate((w3_raw, w4_raw)):
@@ -163,49 +159,36 @@ def tile_picked_cbutter_none_p_kernel(
                     start=start, stop=stop, is_transpose=True,
                 )
 
-        def fetch(label, rows, offsets):
-            term = keep.tile([P, V], F32, name=label, tag=label, align_bytes=64)
-            nc.vector.tensor_copy(term[:], rows[:].indirect(offsets[:]))
-            return term
+        def fetch(term, rows, offsets):
+            nc.vector.tensor_copy(term, rows[:].indirect(offsets[:]))
 
-        sy = sb("sy", [P, PACK - 1, V], F32)
-        ce = sb("ce", [P, PACK - 2, V], F32)
-        yr, er = {}, {}
-
-        def y_terms(t):
-            yr[t] = fetch("yr%d" % t, y[t], right_sb)
-            yl = fetch("yl%d" % t, y[t], left_sb)
+        sy = sb("sy", [P, PACK, V], F32)
+        ce = sb("ce", [P, PACK, V], F32)
+        for t in range(PACK):
+            yr = sb("yr%d" % t, [P, V], F32)
+            yl = sb("yl%d" % t, [P, V], F32)
+            cy = sb("cy%d" % t, [P, V], F32)
+            fetch(yr[:], y[t], right_sb)
+            fetch(yl[:], y[t], left_sb)
             add_turned(t, yl, start=(t == 0))
-            if t < PACK - 1:
-                cy = sb("cy%d" % t, [P, V], F32)
-                nc.gpsimd.tensor_tensor(cy[:], yr[t][:], cw_sb[t], MULT)
-                nc.gpsimd.tensor_tensor(sy[:, t, :], yr[t][:], sw_sb[t], MULT)
-                add_turned(t, cy)
-
-        def e_terms(t):
-            er[t] = fetch("er%d" % t, e[t], right_sb)
-            if t < PACK - 2:
-                se = sb("se%d" % t, [P, V], F32)
-                nc.gpsimd.tensor_tensor(se[:], er[t][:], sw_sb[t], MULT)
-                nc.gpsimd.tensor_tensor(ce[:, t, :], er[t][:], cw_sb[t], MULT)
-                add_turned(t, se)
-
-        y_terms(0)
-        y_terms(1)
-        e_terms(0)
-        y_terms(2)
-        e_terms(1)
-        e_terms(2)
-        y_terms(3)
-        e_terms(3)
-
-        last = keep.tile([P, 6, V], F32, name="last", tag="er1", align_bytes=64)
-        for i, (term, factor) in enumerate(
-            ((er[2], sw_sb[2]), (yr[3], cw_sb[3]), (er[3], sw_sb[3]), (er[2], cw_sb[2]), (er[3], cw_sb[3]), (yr[3], sw_sb[3]))
-        ):
-            nc.vector.tensor_tensor(last[:, i, :], term[:], factor, MULT)
-            if i < 3:
-                add_turned((2, 3, 3)[i], last[:, i, :], stop=(i == 2))
+            nc.gpsimd.tensor_tensor(cy[:], yr[:], cw_sb[t], MULT)
+            nc.gpsimd.tensor_tensor(sy[:, t, :], yr[:], sw_sb[t], MULT)
+            add_turned(t, cy)
+            if t == 1:
+                er_first = sb("er_first", [P, V], F32)
+                se_first = sb("se_first", [P, V], F32)
+                fetch(er_first[:], e[0], right_sb)
+                nc.gpsimd.tensor_tensor(se_first[:], er_first[:], sw_sb[0], MULT)
+                nc.gpsimd.tensor_tensor(ce[:, 0, :], er_first[:], cw_sb[0], MULT)
+                add_turned(0, se_first)
+        er_rest = keep.tile([P, PACK - 1, V], F32, name="er_rest", tag="er_rest", align_bytes=64)
+        se_rest = sb("se_rest", [P, PACK - 1, V], F32)
+        for t in range(1, PACK):
+            fetch(er_rest[:, t - 1, :], e[t], right_sb)
+        nc.vector.tensor_tensor(se_rest[:], er_rest[:], sw_rest[:], MULT)
+        for t in range(1, PACK):
+            add_turned(t, se_rest[:, t - 1, :], stop=(t == PACK - 1))
+        nc.vector.tensor_tensor(ce[:, 1:PACK, :], er_rest[:], cw_rest[:], MULT)
 
         z_grouped = []
         for half in range(2):
@@ -228,20 +211,18 @@ def tile_picked_cbutter_none_p_kernel(
             )
             z_grouped.append(grouped)
 
-        def mix(half):
+        def mix(half, first, count, tag):
             cols = slice(half * HALF, (half + 1) * HALF)
-            mixed = sb("mixed%d" % half, [P, PACK, HALF], F32)
-            nc.vector.tensor_tensor(mixed[:, 0:2, :], ce[:, :, cols], sy[:, 0:2, cols], SUB)
-            nc.vector.tensor_tensor(mixed[:, 2, :], last[:, 3, cols], sy[:, 2, cols], SUB)
-            nc.vector.tensor_tensor(mixed[:, 3, :], last[:, 4, cols], last[:, 5, cols], SUB)
+            mixed = keep.tile([P, count, HALF], F32, name="mixed%d%d" % (half, first), tag=tag, align_bytes=64)
+            tiles = slice(first, first + count)
+            nc.vector.tensor_tensor(mixed[:], ce[:, tiles, cols], sy[:, tiles, cols], SUB)
             return mixed
 
-        def imag_rows(half, mixed, tag):
-            rows = keep.tile([P, PACK, HALF], F32, name="z2_rows%d" % half, tag=tag, align_bytes=64)
+        def imag_rows(rows, half, first, mixed):
             cols = slice(half * HALF // 16, (half + 1) * HALF // 16)
-            for t in range(PACK):
-                nc.vector.tensor_tensor(rows[:, t, :], e[t][:].indirect(left_sb[:, cols]), mixed[:, t, :], ADD)
-            return rows
+            for i in range(mixed.shape[1]):
+                t = first + i
+                nc.vector.tensor_tensor(rows[:, t, :], e[t][:].indirect(left_sb[:, cols]), mixed[:, i, :], ADD)
 
         out_rows = out.rearrange("(a p) v -> p a v", p=P)
 
@@ -257,12 +238,13 @@ def tile_picked_cbutter_none_p_kernel(
                 stop=(part == 1),
             )
 
-        mixed = mix(0)
-        w34_q = quantize("w34", w34_grouped[:], "cw1")
-        rows = imag_rows(0, mixed, "z2_rows0")
+        rows = sb("z2_rows0", [P, PACK, HALF], F32)
+        imag_rows(rows, 0, 0, mix(0, 0, PACK, "mixed0"))
         z2_grouped = keep.tile([P, HALF * PACK], BF16, name="z2_bf16", tag="z2_bf16", align_bytes=64)
         weave(nc.scalar.copy, z2_grouped[:], rows[:])
-        mixed = mix(1)
+        w34_q = quantize("w34", w34_grouped[:], "er_rest")
+        rows = sb("z2_rows1", [P, PACK, HALF], F32)
+        imag_rows(rows, 1, 0, mix(1, 0, 2, "mixed0"))
         z_q = [quantize("z%d" % half, z_grouped[half][:]) for half in range(2)]
         z2_q = quantize("z20", z2_grouped[:])
         result = sb("result0", [P, 4, HALF], F32)
@@ -278,13 +260,13 @@ def tile_picked_cbutter_none_p_kernel(
         accs = [banks[4 + a][:, 0:HALF] for a in range(4)]
         for a in range(4):
             last_pass(accs[a], a, 0, z_q[1])
-        rows = imag_rows(1, mixed, "z2_bf16")
+        imag_rows(rows, 1, 2, mix(1, 2, 2, "z2_bf16"))
         z2_grouped = sb("z21_bf16", [P, HALF * PACK], BF16)
-        weave(nc.vector.tensor_copy, z2_grouped[:], rows[:])
+        weave(nc.scalar.copy, z2_grouped[:, 0 : P * PACK], rows[:, :, 0:P])
+        weave(nc.vector.tensor_copy, z2_grouped[:, P * PACK :], rows[:, :, P:])
         z2_q = quantize("z21", z2_grouped[:])
         result = sb("result1", [P, 4, HALF], F32)
         for a in range(4):
             last_pass(accs[a], a, 1, z2_q)
             (nc.vector.tensor_copy, nc.scalar.copy)[a % 2](result[:, a, :], accs[a])
-            if a % 2 == 1:
-                nc.sync.dma_start(out=out_rows[:, a - 1 : a + 1, HALF:V], in_=result[:, a - 1 : a + 1, :])
+            (nc.sync, nc.scalar)[a % 2].dma_start(out=out_rows[:, a, HALF:V], in_=result[:, a, :])

@@ -54,23 +54,16 @@ def tile_picked_cbutter_none_p_kernel(
             nc.sync.dma_start(out=raw[:], in_=w.rearrange("(p j) c -> p j c", j=PACK)[:, :, lo:hi])
             return raw
 
-        def load_twiddles(first, count):
-            tiles = []
-            for name, src in (("cw", cw), ("sw", sw)):
-                rows = sb("%s%d" % (name, first), [P, count, V], F32)
-                nc.sync.dma_start(out=rows[:], in_=src.rearrange("(p t) v -> p t v", t=PACK)[:, first : first + count, :])
-                tiles.append(rows)
-            return tiles
-
         nc.sync.dma_start(out=word_table[:], in_=x_words[0].rearrange("p n j -> p (n j)").bitcast(I32))
         w1_raw = [load_rows("w1_raw%d" % i, w1, i * H // 2, (i + 1) * H // 2) for i in range(2)]
         w2_raw = [load_rows("w2_raw%d" % i, w2, i * H // 2, (i + 1) * H // 2) for i in range(2)]
         nc.sync.dma_start(right_sb[:], right)
         nc.sync.dma_start(left_sb[:], left)
-        cw_first, sw_first = load_twiddles(0, 1)
-        cw_rest, sw_rest = load_twiddles(1, PACK - 1)
-        cw_sb = [cw_first[:, 0, :]] + [cw_rest[:, i, :] for i in range(PACK - 1)]
-        sw_sb = [sw_first[:, 0, :]] + [sw_rest[:, i, :] for i in range(PACK - 1)]
+        cw_sb = sb("cw_sb", [P, PACK, V], F32)
+        sw_sb = sb("sw_sb", [P, PACK, V], F32)
+        for t in range(PACK):
+            for src, rows in ((cw, cw_sb), (sw, sw_sb)):
+                nc.sync.dma_start(out=rows[:, t, :], in_=src.rearrange("(p t) v -> p t v", t=PACK)[:, t, :])
         w3_raw = load_rows("w3_raw", w3, 0, N)
         w4_raw = load_rows("w4_raw", w4, 0, N)
 
@@ -142,9 +135,9 @@ def tile_picked_cbutter_none_p_kernel(
         y[1] = project("y", 1, w1_q[1], 2, negate)
         codes, scales = quantize("w2", w2_grouped[:])
         w2_q = [(codes[:, s * P : (s + 1) * P], scales[:, s * P : (s + 1) * P]) for s in range(PACK)]
-        e[0] = project("e", 0, w2_q[0], 4, nc.scalar.copy)
-        y[2] = project("y", 2, w1_q[2], 6, negate)
-        y[3] = project("y", 3, w1_q[3], 0, negate)
+        y[2] = project("y", 2, w1_q[2], 4, negate)
+        y[3] = project("y", 3, w1_q[3], 6, negate)
+        e[0] = project("e", 0, w2_q[0], 0, nc.scalar.copy)
         e[1] = project("e", 1, w2_q[1], 2, nc.scalar.copy)
         e[2] = project("e", 2, w2_q[2], 4, nc.scalar.copy)
         e[3] = project("e", 3, w2_q[3], 6, nc.scalar.copy)
@@ -171,24 +164,24 @@ def tile_picked_cbutter_none_p_kernel(
             fetch(yr[:], y[t], right_sb)
             fetch(yl[:], y[t], left_sb)
             add_turned(t, yl, start=(t == 0))
-            nc.gpsimd.tensor_tensor(cy[:], yr[:], cw_sb[t], MULT)
-            nc.gpsimd.tensor_tensor(sy[:, t, :], yr[:], sw_sb[t], MULT)
+            nc.gpsimd.tensor_tensor(cy[:], yr[:], cw_sb[:, t, :], MULT)
+            nc.gpsimd.tensor_tensor(sy[:, t, :], yr[:], sw_sb[:, t, :], MULT)
             add_turned(t, cy)
-            if t == 1:
+            if t == PACK - 1:
                 er_first = sb("er_first", [P, V], F32)
                 se_first = sb("se_first", [P, V], F32)
                 fetch(er_first[:], e[0], right_sb)
-                nc.gpsimd.tensor_tensor(se_first[:], er_first[:], sw_sb[0], MULT)
-                nc.gpsimd.tensor_tensor(ce[:, 0, :], er_first[:], cw_sb[0], MULT)
+                nc.gpsimd.tensor_tensor(se_first[:], er_first[:], sw_sb[:, 0, :], MULT)
+                nc.gpsimd.tensor_tensor(ce[:, 0, :], er_first[:], cw_sb[:, 0, :], MULT)
                 add_turned(0, se_first)
         er_rest = keep.tile([P, PACK - 1, V], F32, name="er_rest", tag="er_rest", align_bytes=64)
         se_rest = sb("se_rest", [P, PACK - 1, V], F32)
         for t in range(1, PACK):
             fetch(er_rest[:, t - 1, :], e[t], right_sb)
-        nc.vector.tensor_tensor(se_rest[:], er_rest[:], sw_rest[:], MULT)
+        nc.vector.tensor_tensor(se_rest[:], er_rest[:], sw_sb[:, 1:PACK, :], MULT)
         for t in range(1, PACK):
             add_turned(t, se_rest[:, t - 1, :], stop=(t == PACK - 1))
-        nc.vector.tensor_tensor(ce[:, 1:PACK, :], er_rest[:], cw_rest[:], MULT)
+        nc.vector.tensor_tensor(ce[:, 1:PACK, :], er_rest[:], cw_sb[:, 1:PACK, :], MULT)
 
         z_grouped = []
         for half in range(2):

from contextlib import ExitStack

import concourse.mybir as mybir
from concourse.masks import make_identity

F32 = mybir.dt.float32
BF16 = mybir.dt.bfloat16
I32 = mybir.dt.int32
U32 = mybir.dt.uint32
U16 = mybir.dt.uint16
U8 = mybir.dt.uint8
FP8X4 = mybir.dt.float8_e4m3fn_x4
MULT = mybir.AluOpType.mult
ADD = mybir.AluOpType.add
SUB = mybir.AluOpType.subtract
COPY = mybir.ActivationFunctionType.Copy

P = 128
PACK = 4
K, T, S, V, N, H = 512, 2048, 1024, 512, 512, 512
BANK = 512
HALF = V // 2
FLOPS = 2 * (2 * K * H * S) + 2 * (2 * H * N * V)


def tile_picked_cbutter_none_p_kernel(
    tc, x_words, x_scales, w1, w2, cw, sw, w3, w4, offs, left, right, out
):
    nc = tc.nc
    with ExitStack() as ctx:
        lists = ctx.enter_context(tc.tile_pool(name="lists", bufs=1))
        keep = ctx.enter_context(tc.tile_pool(name="keep", bufs=1))
        psum = ctx.enter_context(tc.psum_pool(name="psum", bufs=1))

        def sb(name, shape, dtype):
            return keep.tile(shape, dtype, name=name, align_bytes=64)

        banks = [psum.tile([P, BANK], F32, name="bank%d" % b) for b in range(8)]

        offs_sb = lists.tile([P, S // 16], U16, name="offs_sb")
        right_sb = lists.tile([P, V // 16], U16, name="right_sb")
        left_sb = lists.tile([P, V // 16], U16, name="left_sb")
        scale_table = sb("scale_table", [P, T], U8)
        word_table = sb("word_table", [P, T], I32)
        nc.sync.dma_start(offs_sb[:], offs)
        for quad in range(4):
            nc.sync.dma_start(
                out=scale_table[32 * quad : 32 * quad + 32, :].bitcast(I32),
                in_=x_scales[0, 4 * quad : 4 * quad + 4, :].bitcast(I32).unsqueeze(0).to_broadcast([8, 4, T // 4]),
            )

        def load_rows(name, w, lo, hi):
            raw = sb(name, [P, PACK, hi - lo], F32)
            nc.sync.dma_start(out=raw[:], in_=w.rearrange("(p j) c -> p j c", j=PACK)[:, :, lo:hi])
            return raw

        nc.sync.dma_start(out=word_table[:], in_=x_words[0].rearrange("p n j -> p (n j)").bitcast(I32))
        w1_raw = [load_rows("w1_raw%d" % i, w1, i * H // 2, (i + 1) * H // 2) for i in range(2)]
        w2_raw = [load_rows("w2_raw%d" % i, w2, i * H // 2, (i + 1) * H // 2) for i in range(2)]
        nc.sync.dma_start(right_sb[:], right)
        nc.sync.dma_start(left_sb[:], left)
        cw_sb = sb("cw_sb", [P, PACK, V], F32)
        sw_sb = sb("sw_sb", [P, PACK, V], F32)
        for t in range(PACK):
            for src, rows in ((cw, cw_sb), (sw, sw_sb)):
                nc.sync.dma_start(out=rows[:, t, :], in_=src.rearrange("(p t) v -> p t v", t=PACK)[:, t, :])
        w3_raw = load_rows("w3_raw", w3, 0, N)
        w4_raw = load_rows("w4_raw", w4, 0, N)

        identity = sb("identity", [P, P], F32)
        make_identity(nc, identity[:])

        def quantize(name, grouped, tag=None):
            width = grouped.shape[1] // PACK
            codes = keep.tile([P, width], U32, name=name + "_codes", tag=tag or name + "_codes", align_bytes=64)
            scales = sb(name + "_scales", [P, width], U8)
            nc.vector.quantize_mx(out=codes[:].bitcast(FP8X4), scales=scales[:], in_=grouped)
            return codes, scales

        def deal(copy, grouped, raw, first):
            count = raw.shape[2] // PACK
            copy(
                grouped[:].rearrange("p (t m j) -> p m j t", t=PACK, j=PACK)[:, first : first + count],
                raw[:].rearrange("p j (m t) -> p m j t", t=PACK),
            )

        def weave(copy, grouped, rows):
            copy(
                grouped.rearrange("p (c i j) -> p c j i", i=4, j=PACK),
                rows.rearrange("p j (c i) -> p c j i", i=4),
            )

        picked_scales = sb("picked_scales", [P, S], U8)
        nc.vector.tensor_copy(picked_scales[:], scale_table[:].indirect(offs_sb[:]))
        picked_words = []
        for c in range(S // BANK):
            words = sb("picked_words%d" % c, [P, BANK], U32)
            cols = slice(c * BANK // 16, (c + 1) * BANK // 16)
            nc.vector.tensor_copy(words[:], word_table[:].bitcast(U32).indirect(offs_sb[:, cols]))
            picked_words.append(words)

        w1_grouped = sb("w1_bf16", [P, H * PACK], BF16)
        deal(nc.scalar.copy, w1_grouped, w1_raw[0], 0)
        deal(nc.vector.tensor_copy, w1_grouped, w1_raw[1], P // 2)
        w1_q = []
        for first, count in ((0, 1), (1, 1), (2, 2)):
            codes, scales = quantize("w1_%d" % first, w1_grouped[:, first * H : (first + count) * H])
            w1_q.extend((codes[:, i * P : (i + 1) * P], scales[:, i * P : (i + 1) * P]) for i in range(count))

        def negate(dst, src):
            nc.scalar.activation(dst, src, COPY, scale=-1.0)

        def project(name, t, wq, first_bank, copy):
            rows = sb("%s%d" % (name, t), [P, S], F32)
            for c in range(S // BANK):
                bank = banks[first_bank + c]
                cols = slice(c * BANK, (c + 1) * BANK)
                nc.tensor.matmul_mx(
                    out=bank[:],
                    lhsT=wq[0].bitcast(FP8X4),
                    lhsT_scale=wq[1],
                    rhs=picked_words[c][:].bitcast(FP8X4),
                    rhs_scale=picked_scales[:, cols],
                    start=True,
                    stop=True,
                )
                copy(rows[:, cols], bank[:])
            return rows

        w2_grouped = sb("w2_bf16", [P, H * PACK], BF16)
        deal(nc.scalar.copy, w2_grouped, w2_raw[0], 0)
        deal(nc.vector.tensor_copy, w2_grouped, w2_raw[1], P // 2)
        y, e = {}, {}
        y[0] = project("y", 0, w1_q[0], 0, negate)
        y[1] = project("y", 1, w1_q[1], 2, negate)
        codes, scales = quantize("w2", w2_grouped[:])
        w2_q = [(codes[:, s * P : (s + 1) * P], scales[:, s * P : (s + 1) * P]) for s in range(PACK)]
        y[2] = project("y", 2, w1_q[2], 4, negate)
        y[3] = project("y", 3, w1_q[3], 6, negate)
        e[0] = project("e", 0, w2_q[0], 0, nc.scalar.copy)
        e[1] = project("e", 1, w2_q[1], 2, nc.scalar.copy)
        e[2] = project("e", 2, w2_q[2], 4, nc.scalar.copy)
        e[3] = project("e", 3, w2_q[3], 6, nc.scalar.copy)
        w34_grouped = sb("w34_bf16", [P, 2 * N * PACK], BF16)
        for part, raw in enumerate((w3_raw, w4_raw)):
            weave(nc.scalar.copy, w34_grouped[:, part * N * PACK : (part + 1) * N * PACK], raw[:])

        def add_turned(t, term, start=False, stop=False):
            for q in range(4):
                nc.tensor.matmul(
                    banks[4 + q][:, t * P : (t + 1) * P], term[:, q * P : (q + 1) * P], identity[:],
                    start=start, stop=stop, is_transpose=True,
                )

        def fetch(term, rows, offsets):
            nc.vector.tensor_copy(term, rows[:].indirect(offsets[:]))

        sy = sb("sy", [P, PACK, V], F32)
        ce = sb("ce", [P, PACK, V], F32)
        for t in range(PACK):
            yr = sb("yr%d" % t, [P, V], F32)
            yl = sb("yl%d" % t, [P, V], F32)
            cy = sb("cy%d" % t, [P, V], F32)
            fetch(yr[:], y[t], right_sb)
            fetch(yl[:], y[t], left_sb)
            add_turned(t, yl, start=(t == 0))
            nc.gpsimd.tensor_tensor(cy[:], yr[:], cw_sb[:, t, :], MULT)
            nc.gpsimd.tensor_tensor(sy[:, t, :], yr[:], sw_sb[:, t, :], MULT)
            add_turned(t, cy)
            if t == PACK - 1:
                er_first = sb("er_first", [P, V], F32)
                se_first = sb("se_first", [P, V], F32)
                fetch(er_first[:], e[0], right_sb)
                nc.gpsimd.tensor_tensor(se_first[:], er_first[:], sw_sb[:, 0, :], MULT)
                nc.gpsimd.tensor_tensor(ce[:, 0, :], er_first[:], cw_sb[:, 0, :], MULT)
                add_turned(0, se_first)
        er_rest = keep.tile([P, PACK - 1, V], F32, name="er_rest", tag="er_rest", align_bytes=64)
        se_rest = sb("se_rest", [P, PACK - 1, V], F32)
        for t in range(1, PACK):
            fetch(er_rest[:, t - 1, :], e[t], right_sb)
        nc.vector.tensor_tensor(se_rest[:], er_rest[:], sw_sb[:, 1:PACK, :], MULT)
        for t in range(1, PACK):
            add_turned(t, se_rest[:, t - 1, :], stop=(t == PACK - 1))
        nc.vector.tensor_tensor(ce[:, 1:PACK, :], er_rest[:], cw_sb[:, 1:PACK, :], MULT)

        z_grouped = []
        for half in range(2):
            back = banks[half]
            for i in range(2):
                q = 2 * half + i
                turned = sb("turned%d" % q, [P, H], BF16)
                negate(
                    turned[:].rearrange("v (u p e) -> v u p e", u=2, e=2),
                    banks[4 + q][:].rearrange("v (u e p) -> v u p e", u=2, e=2),
                )
                words = turned[:].bitcast(F32)
                for u in range(2):
                    place = (u * 2 + i) * P
                    nc.tensor.transpose(back[:, place : place + P], words[:, u * P : (u + 1) * P], identity[:])
            grouped = sb("z%d_bf16" % half, [P, HALF * PACK], BF16)
            nc.scalar.copy(
                grouped[:].bitcast(F32).rearrange("p (v u) -> p v u", u=2),
                back[:].rearrange("p (u v) -> p v u", u=2),
            )
            z_grouped.append(grouped)

        def mix(half, first, count, tag):
            cols = slice(half * HALF, (half + 1) * HALF)
            mixed = keep.tile([P, count, HALF], F32, name="mixed%d%d" % (half, first), tag=tag, align_bytes=64)
            tiles = slice(first, first + count)
            nc.vector.tensor_tensor(mixed[:], ce[:, tiles, cols], sy[:, tiles, cols], SUB)
            return mixed

        def imag_rows(rows, half, first, mixed):
            cols = slice(half * HALF // 16, (half + 1) * HALF // 16)
            for i in range(mixed.shape[1]):
                t = first + i
                nc.vector.tensor_tensor(rows[:, t, :], e[t][:].indirect(left_sb[:, cols]), mixed[:, i, :], ADD)

        out_rows = out.rearrange("(a p) v -> p a v", p=P)

        def last_pass(acc, a, part, z_q):
            feats = slice(part * N + a * P, part * N + (a + 1) * P)
            nc.tensor.matmul_mx(
                out=acc,
                lhsT=w34_q[0][:, feats].bitcast(FP8X4),
                lhsT_scale=w34_q[1][:, feats],
                rhs=z_q[0][:].bitcast(FP8X4),
                rhs_scale=z_q[1][:],
                start=(part == 0),
                stop=(part == 1),
            )

        rows = sb("z2_rows0", [P, PACK, HALF], F32)
        imag_rows(rows, 0, 0, mix(0, 0, PACK, "mixed0"))
        z2_grouped = keep.tile([P, HALF * PACK], BF16, name="z2_bf16", tag="z2_bf16", align_bytes=64)
        weave(nc.scalar.copy, z2_grouped[:], rows[:])
        w34_q = quantize("w34", w34_grouped[:], "er_rest")
        rows = sb("z2_rows1", [P, PACK, HALF], F32)
        imag_rows(rows, 1, 0, mix(1, 0, 2, "mixed0"))
        z_q = [quantize("z%d" % half, z_grouped[half][:]) for half in range(2)]
        z2_q = quantize("z20", z2_grouped[:])
        result = sb("result0", [P, 4, HALF], F32)
        for a in range(4):
            bank = banks[2 + a // 2]
            acc = bank[:, (a % 2) * HALF : (a % 2 + 1) * HALF]
            last_pass(acc, a, 0, z_q[0])
            last_pass(acc, a, 1, z2_q)
            if a % 2 == 1:
                nc.scalar.copy(result[:, a - 1 : a + 1, :].rearrange("p a v -> p (a v)"), bank[:])
        nc.sync.dma_start(out=out_rows[:, :, 0:HALF], in_=result[:])

        accs = [banks[4 + a][:, 0:HALF] for a in range(4)]
        for a in range(4):
            last_pass(accs[a], a, 0, z_q[1])
        imag_rows(rows, 1, 2, mix(1, 2, 2, "z2_bf16"))
        z2_grouped = sb("z21_bf16", [P, HALF * PACK], BF16)
        weave(nc.scalar.copy, z2_grouped[:, 0 : P * PACK], rows[:, :, 0:P])
        weave(nc.vector.tensor_copy, z2_grouped[:, P * PACK :], rows[:, :, P:])
        z2_q = quantize("z21", z2_grouped[:])
        result = sb("result1", [P, 4, HALF], F32)
        for a in range(4):
            last_pass(accs[a], a, 1, z2_q)
            (nc.vector.tensor_copy, nc.scalar.copy)[a % 2](result[:, a, :], accs[a])
            (nc.sync, nc.scalar)[a % 2].dma_start(out=out_rows[:, a, HALF:V], in_=result[:, a, :])
